import numpy as np
import ml_dtypes


def mxq(x, axis, fmt="e4m3"):
    dtype, down = {"e4m3": (ml_dtypes.float8_e4m3fn, 7), "e5m2": (ml_dtypes.float8_e5m2, 14)}[fmt]
    v = np.moveaxis(np.asarray(x, np.float32).astype(ml_dtypes.bfloat16).astype(np.float64), axis, -1)
    blocks = v.reshape(v.shape[:-1] + (-1, 32))
    amax = np.abs(blocks).max(-1, keepdims=True)
    byte = np.maximum(np.where(amax > 0, np.frexp(amax)[1] - 1 + 127, 0) - down, 1)
    scale = np.exp2(byte - 127.0)
    codes = (blocks / scale).astype(np.float32).astype(dtype).astype(np.float64)
    return np.moveaxis((codes * scale).reshape(v.shape), -1, axis)


WIDE = False


def mx_kscale(k):
    if not WIDE:
        return np.ones(k)
    levels = np.array([10, -10, 5, -5, 0])
    if k % 512:
        return np.exp2(np.random.permutation(np.resize(levels, k // 32))).repeat(32)
    a = np.empty((k // 512, 16))
    for p in range(k // 512):
        a[p, :8] = np.random.permutation(np.resize(levels, 8))
        for g in range(8):
            far = levels[np.abs(levels - a[p, g]) >= 10]
            a[p, g + 8] = far[np.random.randint(len(far))]
    return np.exp2(a.ravel()).repeat(32)


def f64(x):
    return np.asarray(x).astype(np.float64)


def striped(idx):
    return np.tile(idx.reshape(-1, 16).T, (8, 1)).astype(np.uint16)


def unstriped(offs):
    return offs[:16].T.reshape(-1).astype(np.int64)


def pack_weight(w):
    k, n = w.shape
    w = f64(np.asarray(w, np.float32).astype(ml_dtypes.bfloat16)).reshape(k // 32, 32, n)
    amax = np.abs(w).max(1)
    byte = np.clip(np.where(amax > 0, np.frexp(amax)[1] - 1 + 127 - 7, 1), 1, 254)
    scaled = (w * np.exp2(127.0 - byte)[:, None, :]).reshape(k, n).astype(np.float32)
    words = np.ascontiguousarray(scaled.reshape(k // 512, 128, 4, n).transpose(0, 1, 3, 2)).astype(ml_dtypes.float8_e4m3fn).view(np.uint8)
    return words, np.ascontiguousarray(byte.astype(np.uint8).reshape(k // 512, 16, n))


def unpack_weight(words, scales):
    g, p, n, _ = words.shape
    vals = np.ascontiguousarray(words).view(ml_dtypes.float8_e4m3fn).astype(np.float64) * np.repeat(np.exp2(scales.astype(np.float64) - 127.0), 8, axis=1)[..., None]
    return vals.transpose(0, 1, 3, 2).reshape(g * 512, n)


def relu(v):
    return np.maximum(v, 0.0)


K, T, S, D, H, N, V, W = 512, 2048, 1024, 4, 512, 128, 256, 1024
P = 2 ** 7


def setup_inputs():
    n = np.random.standard_normal
    s = mx_kscale(K)[:, None]
    u = mx_kscale(H)
    packed_xT = pack_weight(n((K, T)) * s)
    packed_eT = pack_weight(n((K, W)) * s)
    return {
        "x_words": packed_xT[0],
        "x_scales": packed_xT[1],
        "e_words": packed_eT[0],
        "e_scales": packed_eT[1],
        "w1": (n((K, H)) / np.sqrt(3 * K) / s * u).astype(np.float32),
        "w2": (n((K, H)) / np.sqrt(3 * K) / s * u).astype(np.float32),
        "w3": (n((K, H)) / np.sqrt(3 * K) / s * u).astype(np.float32),
        "in1": (np.tile((np.arange(S) % 4 >= 1) * 1.0, (P, 1))).astype(np.float32),
        "in2": (np.tile((np.arange(S) % 4 >= 2) * 1.0, (P, 1))).astype(np.float32),
        "pw": (np.tile(n(S) * 0.7, (P, 1))).astype(np.float32),
        "w4": (n((H, N)) / np.sqrt(3 * H) / u[:, None]).astype(np.float32),
        "w5": (n((H, N)) / np.sqrt(3 * H) / u[:, None]).astype(np.float32),
        "w6": (n((K, N)) / np.sqrt(3 * K) / s).astype(np.float32),
        "offs": striped(np.random.permutation(T)[:S]),
        "user": striped(np.random.permutation(W)[:V]),
    }


def reference(x_words, x_scales, e_words, e_scales, w1, w2, w3, in1, in2, pw, w4, w5, w6, offs, user):
    xq = unpack_weight(x_words, x_scales)[:, unstriped(offs)]
    y0 = mxq(f64(w1), 0, "e4m3").T @ xq
    y1 = mxq(f64(w2), 0, "e4m3").T @ xq
    y2 = mxq(f64(w3), 0, "e4m3").T @ xq
    z = relu(y0 + (np.pad(y1, ((0, 0), (1, 0)))[:, :S]) * f64(in1)[:1] + (np.pad(y2, ((0, 0), (2, 0)))[:, :S]) * f64(in2)[:1])
    hp = z.reshape(len(z), -1, D).max(axis=2)
    yw = y0 * f64(pw)[:1]
    vp = yw.reshape(len(yw), -1, D).sum(axis=2)
    e_user = unpack_weight(e_words, e_scales)[:, unstriped(user)]
    return relu(mxq(f64(w4), 0, "e4m3").T @ mxq(hp, 0, "e4m3") + mxq(f64(w5), 0, "e4m3").T @ mxq(vp, 0, "e4m3") + mxq(f64(w6), 0, "e4m3").T @ e_user)

@@ -1,0 +1,243 @@
+from contextlib import ExitStack
+
+import concourse.mybir as mybir
+from concourse.masks import make_identity
+
+K, T, S, D, H, N, V, W = 512, 2048, 1024, 4, 512, 128, 256, 1024
+FLOPS = 2 * (3 * K * H * S + 2 * H * N * V + K * N * V)
+
+F32 = mybir.dt.float32
+BF16 = mybir.dt.bfloat16
+I32 = mybir.dt.int32
+U32 = mybir.dt.uint32
+U16 = mybir.dt.uint16
+U8 = mybir.dt.uint8
+FP8X4 = mybir.dt.float8_e4m3fn_x4
+MULT, ADD, MAX = mybir.AluOpType.mult, mybir.AluOpType.add, mybir.AluOpType.max
+COPY, RELU = mybir.ActivationFunctionType.Copy, mybir.ActivationFunctionType.Relu
+
+P = 128
+PACK = 4
+TAPS = 3
+BACK = TAPS - 1
+BLOCKS = V // P
+LEAD_WORDS = 8
+LEAD_BYTES = 32
+
+
+def tile_picked_ycaser_relu_p_kernel(
+    tc, x_words, x_scales, e_words, e_scales, w1, w2, w3, in1, in2, pw, w4, w5, w6, offs, user, out
+):
+    nc = tc.nc
+    with ExitStack() as ctx:
+        lists = ctx.enter_context(tc.tile_pool(name="lists", bufs=1))
+        keep = ctx.enter_context(tc.tile_pool(name="keep", bufs=1))
+        ring = ctx.enter_context(tc.tile_pool(name="ring", bufs=3))
+        psum = ctx.enter_context(tc.psum_pool(name="psum", bufs=1))
+
+        def kept(name, shape, dtype):
+            return keep.tile(shape, dtype, name=name, align_bytes=64)
+
+        def load_words(name, words, width):
+            tile = kept(name, [P, width], U32)
+            nc.sync.dma_start(out=tile[:].bitcast(I32), in_=words[0].rearrange("p n t -> p (n t)").bitcast(I32))
+            return tile
+
+        def load_scales(queue, tile, scales):
+            for q in range(4):
+                queue.dma_start(
+                    out=tile[32 * q : 32 * q + 4, :].bitcast(I32), in_=scales[0, 4 * q : 4 * q + 4, :].bitcast(I32)
+                )
+
+        def load_scales_all(queue, tile, scales):
+            for q in range(4):
+                rows = scales[0, 4 * q : 4 * q + 4, :].bitcast(I32)
+                queue.dma_start(
+                    out=tile[32 * q : 32 * q + 32, :].bitcast(I32), in_=rows.partition_broadcast(8)
+                )
+
+        def load_weight(name, w):
+            tile = kept(name, [P, PACK, w.shape[1]], F32)
+            nc.sync.dma_start(out=tile[:], in_=w.rearrange("(p j) c -> p j c", j=PACK))
+            return tile
+
+        def load_factor(name, rows):
+            tile = kept(name, [P, BLOCKS, D], F32)
+            nc.gpsimd.dma_start(out=tile[:], in_=rows[0, :].rearrange("(b p d) -> p b d", p=P, d=D))
+            return tile
+
+        def interleave(name, raw):
+            width = raw.shape[2]
+            grouped = kept(name, [P, width * PACK], BF16)
+            nc.scalar.activation(
+                out=grouped[:].rearrange("p (c i j) -> p c j i", i=4, j=PACK),
+                in_=raw[:].rearrange("p j (c i) -> p c j i", i=4),
+                func=COPY,
+            )
+            return grouped
+
+        def quantise(name, grouped):
+            width = grouped.shape[1] // PACK
+            codes = kept(name + "_codes", [P, width], U32)
+            scales = kept(name + "_scales", [P, width], U8)
+            nc.vector.quantize_mx(out=codes[:].bitcast(FP8X4), scales=scales[:], in_=grouped[:])
+            return codes, scales
+
+        def mx(dst, lhs, rhs, start, stop):
+            nc.tensor.matmul_mx(
+                out=dst,
+                lhsT=lhs[0].bitcast(FP8X4),
+                lhsT_scale=lhs[1],
+                rhs=rhs[0].bitcast(FP8X4),
+                rhs_scale=rhs[1],
+                start=start,
+                stop=stop,
+            )
+
+        x_scale_tab = kept("x_scale_tab", [P, T], U8)
+        e_scale_tab = kept("e_scale_tab", [P, W], U8)
+        x_got_words = kept("x_got_words", [P, LEAD_WORDS + S], U32)
+        x_got_scales = kept("x_got_scales", [P, LEAD_BYTES + S], U8)
+        nc.vector.memset(e_scale_tab[:].bitcast(I32), 0)
+        nc.vector.memset(x_got_words[:, :LEAD_WORDS].bitcast(I32), 0)
+        nc.vector.memset(x_got_scales[:, :LEAD_BYTES].bitcast(I32), 0)
+
+        item_list = lists.tile([P, S // 16], U16, name="item_list")
+        user_list = lists.tile([P, V // 16], U16, name="user_list")
+        nc.sync.dma_start(item_list[:], offs)
+        load_scales_all(nc.sync, x_scale_tab, x_scales)
+        w1_raw = load_weight("w1_raw", w1)
+        x_word_tab = load_words("x_word_tab", x_words, T)
+        w2_raw = load_weight("w2_raw", w2)
+        in1_col = load_factor("in1_col", in1)
+        pw_col = load_factor("pw_col", pw)
+        in2_col = load_factor("in2_col", in2)
+        nc.sync.dma_start(user_list[:], user)
+        load_scales(nc.sync, e_scale_tab, e_scales)
+        e_word_tab = load_words("e_word_tab", e_words, W)
+        w3_raw = load_weight("w3_raw", w3)
+        w6_raw = load_weight("w6_raw", w6)
+        w5_raw = load_weight("w5_raw", w5)
+        w4_raw = load_weight("w4_raw", w4)
+
+        eye_f32 = kept("eye_f32", [P, P], F32)
+        eye_bf16 = kept("eye_bf16", [P, P], BF16)
+        make_identity(nc, eye_f32[:])
+        make_identity(nc, eye_bf16[:])
+
+        x_codes = kept("x_codes", [P, D + BACK, V], U32)
+        x_planes = kept("x_planes", [P, D + BACK, V], U8)
+        for table, got, lead, dealt in (
+            (x_scale_tab, x_got_scales, LEAD_BYTES, x_planes),
+            (x_word_tab, x_got_words, LEAD_WORDS, x_codes),
+        ):
+            nc.vector.tensor_copy(got[:, lead:], table[:].indirect(item_list[:]))
+            nc.vector.tensor_copy(dealt[:, BACK:, :], got[:, lead:].rearrange("p (v d) -> p d v", d=D))
+            earlier = got[:, lead - D : lead - D + S].rearrange("p (v d) -> p d v", d=D)
+            nc.vector.tensor_copy(dealt[:, :BACK, :], earlier[:, D - BACK :, :])
+
+        taps = {}
+
+        def prepare(store, name, raw):
+            codes, scales = quantise(name, interleave(name + "_bf16", raw))
+            store[name] = (codes[:], scales[:])
+
+        e_codes = kept("e_codes", [P, V], U32)
+        e_planes = kept("e_planes", [P, V], U8)
+        heads = {}
+
+        def by_slot(bank):
+            return bank[:].rearrange("p (m t) -> p t m", t=PACK)
+
+        def product(name, back, b, d):
+            users = slice(b * P, (b + 1) * P)
+            bank = psum.tile([P, H], F32, name=f"y{back}", bufs=2)
+            plane = d + BACK - back
+            mx(bank[:], (x_codes[:, plane, users], x_planes[:, plane, users]), taps[name], True, True)
+            return bank
+
+        def first_tap(b, d):
+            bank = product("w1", 0, b, d)
+            y0 = ring.tile([P, PACK, P], F32, name="y0_sb")
+            yw = ring.tile([P, PACK, P], F32, name="yw", bufs=4)
+            nc.scalar.activation(out=y0[:], in_=by_slot(bank), func=COPY)
+            nc.gpsimd.tensor_scalar(
+                out=yw[:], in0=y0[:], scalar1=pw_col[:, b, d : d + 1], scalar2=0.0, op0=MULT, op1=ADD
+            )
+            return y0, yw
+
+        def second_tap(b, d, y0):
+            bank = product("w2", 1, b, d)
+            y01 = ring.tile([P, PACK, P], F32, name="y01")
+            nc.vector.scalar_tensor_tensor(
+                out=y01[:], in0=by_slot(bank), scalar=in1_col[:, b, d : d + 1], in1=y0[:], op0=MULT, op1=ADD
+            )
+            return y01
+
+        def third_tap(b, d, y01, best):
+            bank = product("w3", 2, b, d)
+            z = ring.tile([P, PACK, P], BF16, name="z")
+            nc.vector.scalar_tensor_tensor(
+                out=z[:], in0=by_slot(bank), scalar=in2_col[:, b, d : d + 1], in1=y01[:], op0=MULT, op1=ADD
+            )
+            if best is None:
+                return z
+            larger = ring.tile([P, PACK, P], BF16, name="larger")
+            nc.vector.tensor_tensor(out=larger[:], in0=best[:], in1=z[:], op=MAX)
+            return larger
+
+        def add_turned(d, yw, vp_bank):
+            for t in range(PACK):
+                nc.tensor.matmul(
+                    vp_bank[:, t, :], yw[:, t, :], eye_f32[:],
+                    start=(d == 0 and t == 0), stop=(d == D - 1 and t == PACK - 1), is_transpose=True,
+                )
+
+        def head(b, best, vp_bank):
+            users = slice(b * P, (b + 1) * P)
+            vp_bf16 = kept(f"vp_bf16_{b}", [P, P * PACK], BF16)
+            nc.scalar.activation(
+                out=vp_bf16[:].rearrange("p (v t) -> p v t", t=PACK), in_=vp_bank[:].rearrange("p t v -> p v t"), func=COPY
+            )
+            vp_q = quantise(f"vp{b}", vp_bf16)
+            hp_bank = psum.tile([P, PACK, P], BF16, name="tail")
+            for t in range(PACK):
+                nc.tensor.transpose(hp_bank[:, t, :], best[:, t, :], eye_bf16[:])
+            hp_bf16 = kept(f"hp_bf16_{b}", [P, P * PACK], BF16)
+            nc.scalar.activation(
+                out=hp_bf16[:].rearrange("p (v t) -> p v t", t=PACK), in_=hp_bank[:].rearrange("p t v -> p v t"), func=RELU
+            )
+            hp_q = quantise(f"hp{b}", hp_bf16)
+            out_bank = psum.tile([P, P], F32, name="tail")
+            mx(out_bank[:], heads["w6"], (e_codes[:, users], e_planes[:, users]), True, False)
+            mx(out_bank[:], heads["w5"], (vp_q[0][:], vp_q[1][:]), False, False)
+            mx(out_bank[:], heads["w4"], (hp_q[0][:], hp_q[1][:]), False, True)
+            result = kept(f"result{b}", [P, P], F32)
+            nc.scalar.activation(out=result[:], in_=out_bank[:], func=RELU)
+            nc.sync.dma_start(out=out[:, users], in_=result[:])
+
+        steps = [(b, d) for b in range(BLOCKS) for d in range(D)]
+        prepare(taps, "w1", w1_raw)
+        nc.vector.tensor_copy(e_planes[:], e_scale_tab[:].indirect(user_list[:]))
+        nc.vector.tensor_copy(e_codes[:], e_word_tab[:].indirect(user_list[:]))
+        prepare(taps, "w2", w2_raw)
+        firsts = [first_tap(*steps[0]), first_tap(*steps[1])]
+        prepare(taps, "w3", w3_raw)
+        seconds = [second_tap(*steps[0], firsts[0][0])]
+        best = None
+        vp_bank = None
+        for n, (b, d) in enumerate(steps):
+            if n + 1 < len(steps):
+                seconds.append(second_tap(*steps[n + 1], firsts[n + 1][0]))
+            if n + 2 < len(steps):
+                firsts.append(first_tap(*steps[n + 2]))
+            if d == 0:
+                best = None
+                vp_bank = psum.tile([P, PACK, P], F32, name="vp")
+            add_turned(d, firsts[n][1], vp_bank)
+            best = third_tap(b, d, seconds[n], best)
+            if n == 1:
+                for name, raw in (("w6", w6_raw), ("w5", w5_raw), ("w4", w4_raw)):
+                    prepare(heads, name, raw)
+            if d == D - 1:
+                head(b, best, vp_bank)

@@ -63,17 +63,18 @@ def tile_picked_ycaser_relu_p_kernel(
 
         def load_factor(name, rows):
             tile = kept(name, [P, BLOCKS, D], F32)
-            nc.gpsimd.dma_start(out=tile[:], in_=rows[0, :].rearrange("(b p d) -> p b d", p=P, d=D))
+            nc.sync.dma_start(out=tile[:], in_=rows[0, :].rearrange("(b p d) -> p b d", p=P, d=D))
             return tile
 
-        def interleave(name, raw):
+        def interleave(name, raw, on_vector):
             width = raw.shape[2]
             grouped = kept(name, [P, width * PACK], BF16)
-            nc.scalar.activation(
-                out=grouped[:].rearrange("p (c i j) -> p c j i", i=4, j=PACK),
-                in_=raw[:].rearrange("p j (c i) -> p c j i", i=4),
-                func=COPY,
-            )
+            dst = grouped[:].rearrange("p (c i j) -> p c j i", i=4, j=PACK)
+            src = raw[:].rearrange("p j (c i) -> p c j i", i=4)
+            split = (width - on_vector) // 4
+            nc.scalar.activation(out=dst[:, :split], in_=src[:, :split], func=COPY)
+            if on_vector:
+                nc.vector.tensor_copy(out=dst[:, split:], in_=src[:, split:])
             return grouped
 
         def quantise(name, grouped):
@@ -106,16 +107,16 @@ def tile_picked_ycaser_relu_p_kernel(
         user_list = lists.tile([P, V // 16], U16, name="user_list")
         nc.sync.dma_start(item_list[:], offs)
         load_scales_all(nc.sync, x_scale_tab, x_scales)
-        w1_raw = load_weight("w1_raw", w1)
         x_word_tab = load_words("x_word_tab", x_words, T)
+        w1_raw = load_weight("w1_raw", w1)
         w2_raw = load_weight("w2_raw", w2)
         in1_col = load_factor("in1_col", in1)
         pw_col = load_factor("pw_col", pw)
         in2_col = load_factor("in2_col", in2)
         nc.sync.dma_start(user_list[:], user)
-        load_scales(nc.sync, e_scale_tab, e_scales)
         e_word_tab = load_words("e_word_tab", e_words, W)
         w3_raw = load_weight("w3_raw", w3)
+        load_scales(nc.sync, e_scale_tab, e_scales)
         w6_raw = load_weight("w6_raw", w6)
         w5_raw = load_weight("w5_raw", w5)
         w4_raw = load_weight("w4_raw", w4)
@@ -138,8 +139,8 @@ def tile_picked_ycaser_relu_p_kernel(
 
         taps = {}
 
-        def prepare(store, name, raw):
-            codes, scales = quantise(name, interleave(name + "_bf16", raw))
+        def prepare(store, name, raw, on_vector=0):
+            codes, scales = quantise(name, interleave(name + "_bf16", raw, on_vector))
             store[name] = (codes[:], scales[:])
 
         e_codes = kept("e_codes", [P, V], U32)
@@ -158,13 +159,14 @@ def tile_picked_ycaser_relu_p_kernel(
 
         def first_tap(b, d):
             bank = product("w1", 0, b, d)
-            y0 = ring.tile([P, PACK, P], F32, name="y0_sb")
-            yw = ring.tile([P, PACK, P], F32, name="yw", bufs=4)
+            y0 = ring.tile([P, PACK, P], F32, name="y0_sb", bufs=5)
             nc.scalar.activation(out=y0[:], in_=by_slot(bank), func=COPY)
-            nc.gpsimd.tensor_scalar(
-                out=yw[:], in0=y0[:], scalar1=pw_col[:, b, d : d + 1], scalar2=0.0, op0=MULT, op1=ADD
-            )
-            return y0, yw
+            return y0
+
+        def weigh(b, d, y0):
+            yw = ring.tile([P, PACK, P], F32, name="yw", bufs=4)
+            nc.scalar.activation(out=yw[:], in_=y0[:], func=COPY, scale=pw_col[:, b, d : d + 1])
+            return yw
 
         def second_tap(b, d, y0):
             bank = product("w2", 1, b, d)
@@ -186,11 +188,12 @@ def tile_picked_ycaser_relu_p_kernel(
             nc.vector.tensor_tensor(out=larger[:], in0=best[:], in1=z[:], op=MAX)
             return larger
 
-        def add_turned(d, yw, vp_bank):
-            for t in range(PACK):
+        def add_turned(d, pair, vp_bank):
+            turns = [(yw, t) for yw in pair for t in range(PACK)]
+            for n, (yw, t) in enumerate(turns):
                 nc.tensor.matmul(
                     vp_bank[:, t, :], yw[:, t, :], eye_f32[:],
-                    start=(d == 0 and t == 0), stop=(d == D - 1 and t == PACK - 1), is_transpose=True,
+                    start=(d == 1 and n == 0), stop=(d == D - 1 and n == len(turns) - 1), is_transpose=True,
                 )
 
         def head(b, best, vp_bank):
@@ -200,6 +203,9 @@ def tile_picked_ycaser_relu_p_kernel(
                 out=vp_bf16[:].rearrange("p (v t) -> p v t", t=PACK), in_=vp_bank[:].rearrange("p t v -> p v t"), func=COPY
             )
             vp_q = quantise(f"vp{b}", vp_bf16)
+            out_bank = psum.tile([P, P], F32, name="vp")
+            mx(out_bank[:], heads["w6"], (e_codes[:, users], e_planes[:, users]), True, False)
+            mx(out_bank[:], heads["w5"], (vp_q[0][:], vp_q[1][:]), False, False)
             hp_bank = psum.tile([P, PACK, P], BF16, name="tail")
             for t in range(PACK):
                 nc.tensor.transpose(hp_bank[:, t, :], best[:, t, :], eye_bf16[:])
@@ -208,9 +214,6 @@ def tile_picked_ycaser_relu_p_kernel(
                 out=hp_bf16[:].rearrange("p (v t) -> p v t", t=PACK), in_=hp_bank[:].rearrange("p t v -> p v t"), func=RELU
             )
             hp_q = quantise(f"hp{b}", hp_bf16)
-            out_bank = psum.tile([P, P], F32, name="tail")
-            mx(out_bank[:], heads["w6"], (e_codes[:, users], e_planes[:, users]), True, False)
-            mx(out_bank[:], heads["w5"], (vp_q[0][:], vp_q[1][:]), False, False)
             mx(out_bank[:], heads["w4"], (hp_q[0][:], hp_q[1][:]), False, True)
             result = kept(f"result{b}", [P, P], F32)
             nc.scalar.activation(out=result[:], in_=out_bank[:], func=RELU)
@@ -218,25 +221,29 @@ def tile_picked_ycaser_relu_p_kernel(
 
         steps = [(b, d) for b in range(BLOCKS) for d in range(D)]
         prepare(taps, "w1", w1_raw)
-        nc.vector.tensor_copy(e_planes[:], e_scale_tab[:].indirect(user_list[:]))
         nc.vector.tensor_copy(e_codes[:], e_word_tab[:].indirect(user_list[:]))
         prepare(taps, "w2", w2_raw)
         firsts = [first_tap(*steps[0]), first_tap(*steps[1])]
-        prepare(taps, "w3", w3_raw)
-        seconds = [second_tap(*steps[0], firsts[0][0])]
+        seconds = [second_tap(*steps[0], firsts[0])]
+        prepare(taps, "w3", w3_raw, on_vector=H // 2)
+        weighed = []
         best = None
         vp_bank = None
         for n, (b, d) in enumerate(steps):
             if n + 1 < len(steps):
-                seconds.append(second_tap(*steps[n + 1], firsts[n + 1][0]))
+                seconds.append(second_tap(*steps[n + 1], firsts[n + 1]))
             if n + 2 < len(steps):
                 firsts.append(first_tap(*steps[n + 2]))
+            weighed.append(weigh(b, d, firsts[n]))
             if d == 0:
                 best = None
+            if d == 1:
                 vp_bank = psum.tile([P, PACK, P], F32, name="vp")
-            add_turned(d, firsts[n][1], vp_bank)
+            if d % 2 == 1:
+                add_turned(d, (weighed[n], weighed[n - 1]), vp_bank)
             best = third_tap(b, d, seconds[n], best)
             if n == 1:
+                nc.vector.tensor_copy(e_planes[:], e_scale_tab[:].indirect(user_list[:]))
                 for name, raw in (("w6", w6_raw), ("w5", w5_raw), ("w4", w4_raw)):
                     prepare(heads, name, raw)
             if d == D - 1:

@@ -49,13 +49,6 @@ def tile_picked_ycaser_relu_p_kernel(
                     out=tile[32 * q : 32 * q + 4, :].bitcast(I32), in_=scales[0, 4 * q : 4 * q + 4, :].bitcast(I32)
                 )
 
-        def load_scales_all(queue, tile, scales):
-            for q in range(4):
-                rows = scales[0, 4 * q : 4 * q + 4, :].bitcast(I32)
-                queue.dma_start(
-                    out=tile[32 * q : 32 * q + 32, :].bitcast(I32), in_=rows.partition_broadcast(8)
-                )
-
         def load_weight(name, w):
             tile = kept(name, [P, PACK, w.shape[1]], F32)
             nc.sync.dma_start(out=tile[:], in_=w.rearrange("(p j) c -> p j c", j=PACK))
@@ -66,15 +59,13 @@ def tile_picked_ycaser_relu_p_kernel(
             nc.sync.dma_start(out=tile[:], in_=rows[0, :].rearrange("(b p d) -> p b d", p=P, d=D))
             return tile
 
-        def interleave(name, raw, on_vector):
+        def interleave(name, raw, dealt):
             width = raw.shape[2]
             grouped = kept(name, [P, width * PACK], BF16)
-            dst = grouped[:].rearrange("p (c i j) -> p c j i", i=4, j=PACK)
-            src = raw[:].rearrange("p j (c i) -> p c j i", i=4)
-            split = (width - on_vector) // 4
-            nc.scalar.activation(out=dst[:, :split], in_=src[:, :split], func=COPY)
-            if on_vector:
-                nc.vector.tensor_copy(out=dst[:, split:], in_=src[:, split:])
+            order = "p (i c j) -> p c j i" if dealt else "p (c i j) -> p c j i"
+            nc.scalar.activation(
+                out=grouped[:].rearrange(order, i=4, j=PACK), in_=raw[:].rearrange("p j (c i) -> p c j i", i=4), func=COPY
+            )
             return grouped
 
         def quantise(name, grouped):
@@ -99,6 +90,7 @@ def tile_picked_ycaser_relu_p_kernel(
         e_scale_tab = kept("e_scale_tab", [P, W], U8)
         x_got_words = kept("x_got_words", [P, LEAD_WORDS + S], U32)
         x_got_scales = kept("x_got_scales", [P, LEAD_BYTES + S], U8)
+        nc.gpsimd.memset(x_scale_tab[:].bitcast(I32), 0)
         nc.vector.memset(e_scale_tab[:].bitcast(I32), 0)
         nc.vector.memset(x_got_words[:, :LEAD_WORDS].bitcast(I32), 0)
         nc.vector.memset(x_got_scales[:, :LEAD_BYTES].bitcast(I32), 0)
@@ -106,16 +98,16 @@ def tile_picked_ycaser_relu_p_kernel(
         item_list = lists.tile([P, S // 16], U16, name="item_list")
         user_list = lists.tile([P, V // 16], U16, name="user_list")
         nc.sync.dma_start(item_list[:], offs)
-        load_scales_all(nc.sync, x_scale_tab, x_scales)
         x_word_tab = load_words("x_word_tab", x_words, T)
+        load_scales(nc.sync, x_scale_tab, x_scales)
         w1_raw = load_weight("w1_raw", w1)
         w2_raw = load_weight("w2_raw", w2)
         in1_col = load_factor("in1_col", in1)
         pw_col = load_factor("pw_col", pw)
         in2_col = load_factor("in2_col", in2)
         nc.sync.dma_start(user_list[:], user)
-        e_word_tab = load_words("e_word_tab", e_words, W)
         w3_raw = load_weight("w3_raw", w3)
+        e_word_tab = load_words("e_word_tab", e_words, W)
         load_scales(nc.sync, e_scale_tab, e_scales)
         w6_raw = load_weight("w6_raw", w6)
         w5_raw = load_weight("w5_raw", w5)
@@ -128,19 +120,20 @@ def tile_picked_ycaser_relu_p_kernel(
 
         x_codes = kept("x_codes", [P, D + BACK, V], U32)
         x_planes = kept("x_planes", [P, D + BACK, V], U8)
-        for table, got, lead, dealt in (
-            (x_scale_tab, x_got_scales, LEAD_BYTES, x_planes),
-            (x_word_tab, x_got_words, LEAD_WORDS, x_codes),
+        for table, got, lead, dealt, run in (
+            (x_word_tab, x_got_words, LEAD_WORDS, x_codes, 4),
+            (x_scale_tab, x_got_scales, LEAD_BYTES, x_planes, 16),
         ):
             nc.vector.tensor_copy(got[:, lead:], table[:].indirect(item_list[:]))
-            nc.vector.tensor_copy(dealt[:, BACK:, :], got[:, lead:].rearrange("p (v d) -> p d v", d=D))
-            earlier = got[:, lead - D : lead - D + S].rearrange("p (v d) -> p d v", d=D)
-            nc.vector.tensor_copy(dealt[:, :BACK, :], earlier[:, D - BACK :, :])
+            planes = dealt[:].rearrange("p e (c i) -> p c e i", i=run)
+            nc.vector.tensor_copy(planes[:, :, BACK:], got[:, lead:].rearrange("p (c i d) -> p c d i", i=run, d=D))
+            earlier = got[:, lead - D : lead - D + S].rearrange("p (c i d) -> p c d i", i=run, d=D)
+            nc.vector.tensor_copy(planes[:, :, :BACK], earlier[:, :, D - BACK :])
 
         taps = {}
 
-        def prepare(store, name, raw, on_vector=0):
-            codes, scales = quantise(name, interleave(name + "_bf16", raw, on_vector))
+        def prepare(store, name, raw, dealt):
+            codes, scales = quantise(name, interleave(name + "_bf16", raw, dealt))
             store[name] = (codes[:], scales[:])
 
         e_codes = kept("e_codes", [P, V], U32)
@@ -148,7 +141,7 @@ def tile_picked_ycaser_relu_p_kernel(
         heads = {}
 
         def by_slot(bank):
-            return bank[:].rearrange("p (m t) -> p t m", t=PACK)
+            return bank[:].rearrange("p (t m) -> p t m", t=PACK)
 
         def product(name, back, b, d):
             users = slice(b * P, (b + 1) * P)
@@ -170,20 +163,21 @@ def tile_picked_ycaser_relu_p_kernel(
 
         def second_tap(b, d, y0):
             bank = product("w2", 1, b, d)
-            y01 = ring.tile([P, PACK, P], F32, name="y01")
+            y01 = ring.tile([P, PACK, P], F32, name="y01", bufs=4)
             nc.vector.scalar_tensor_tensor(
                 out=y01[:], in0=by_slot(bank), scalar=in1_col[:, b, d : d + 1], in1=y0[:], op0=MULT, op1=ADD
             )
             return y01
 
-        def third_tap(b, d, y01, best):
+        def third_tap(b, d, y01):
             bank = product("w3", 2, b, d)
-            z = ring.tile([P, PACK, P], BF16, name="z")
+            z = ring.tile([P, PACK, P], BF16, name="z", bufs=4)
             nc.vector.scalar_tensor_tensor(
                 out=z[:], in0=by_slot(bank), scalar=in2_col[:, b, d : d + 1], in1=y01[:], op0=MULT, op1=ADD
             )
-            if best is None:
-                return z
+            return z
+
+        def larger_of(best, z):
             larger = ring.tile([P, PACK, P], BF16, name="larger")
             nc.vector.tensor_tensor(out=larger[:], in0=best[:], in1=z[:], op=MAX)
             return larger
@@ -220,31 +214,31 @@ def tile_picked_ycaser_relu_p_kernel(
             nc.sync.dma_start(out=out[:, users], in_=result[:])
 
         steps = [(b, d) for b in range(BLOCKS) for d in range(D)]
-        prepare(taps, "w1", w1_raw)
+        prepare(taps, "w1", w1_raw, True)
+        prepare(taps, "w2", w2_raw, True)
         nc.vector.tensor_copy(e_codes[:], e_word_tab[:].indirect(user_list[:]))
-        prepare(taps, "w2", w2_raw)
-        firsts = [first_tap(*steps[0]), first_tap(*steps[1])]
-        seconds = [second_tap(*steps[0], firsts[0])]
-        prepare(taps, "w3", w3_raw, on_vector=H // 2)
+        nc.vector.tensor_copy(e_planes[:], e_scale_tab[:].indirect(user_list[:]))
+        prepare(taps, "w3", w3_raw, True)
+        firsts = [first_tap(*steps[n]) for n in range(2)]
+        seconds = [second_tap(*steps[n], firsts[n]) for n in range(2)]
         weighed = []
+        thirds = []
         best = None
         vp_bank = None
         for n, (b, d) in enumerate(steps):
-            if n + 1 < len(steps):
-                seconds.append(second_tap(*steps[n + 1], firsts[n + 1]))
             if n + 2 < len(steps):
                 firsts.append(first_tap(*steps[n + 2]))
             weighed.append(weigh(b, d, firsts[n]))
-            if d == 0:
-                best = None
             if d == 1:
                 vp_bank = psum.tile([P, PACK, P], F32, name="vp")
             if d % 2 == 1:
                 add_turned(d, (weighed[n], weighed[n - 1]), vp_bank)
-            best = third_tap(b, d, seconds[n], best)
+            thirds.append(third_tap(b, d, seconds[n]))
+            if n + 2 < len(steps):
+                seconds.append(second_tap(*steps[n + 2], firsts[n + 2]))
+            best = thirds[n] if d == 0 else larger_of(best, thirds[n])
             if n == 1:
-                nc.vector.tensor_copy(e_planes[:], e_scale_tab[:].indirect(user_list[:]))
                 for name, raw in (("w6", w6_raw), ("w5", w5_raw), ("w4", w4_raw)):
-                    prepare(heads, name, raw)
+                    prepare(heads, name, raw, False)
             if d == D - 1:
                 head(b, best, vp_bank)

@@ -18,11 +18,14 @@ COPY, RELU = mybir.ActivationFunctionType.Copy, mybir.ActivationFunctionType.Rel
 
 P = 128
 PACK = 4
-TAPS = 3
-BACK = TAPS - 1
+QUADRANT = 32
+LIST_ROWS = 16
+BACK = 2
 BLOCKS = V // P
-LEAD_WORDS = 8
-LEAD_BYTES = 32
+LINE = 16
+LEAD = 32
+AHEAD = 2
+TAP_BANKS = 2
 
 
 def tile_picked_ycaser_relu_p_kernel(
@@ -36,17 +39,18 @@ def tile_picked_ycaser_relu_p_kernel(
         psum = ctx.enter_context(tc.psum_pool(name="psum", bufs=1))
 
         def kept(name, shape, dtype):
-            return keep.tile(shape, dtype, name=name, align_bytes=64)
+            return keep.tile(shape, dtype, name=name, tag=name, align_bytes=64)
 
         def load_words(name, words, width):
             tile = kept(name, [P, width], U32)
             nc.sync.dma_start(out=tile[:].bitcast(I32), in_=words[0].rearrange("p n t -> p (n t)").bitcast(I32))
             return tile
 
-        def load_scales(queue, tile, scales):
-            for q in range(4):
-                queue.dma_start(
-                    out=tile[32 * q : 32 * q + 4, :].bitcast(I32), in_=scales[0, 4 * q : 4 * q + 4, :].bitcast(I32)
+        def load_scales(tile, scales):
+            for q in range(P // QUADRANT):
+                nc.sync.dma_start(
+                    out=tile[QUADRANT * q : QUADRANT * q + 4, :].bitcast(I32),
+                    in_=scales[0, 4 * q : 4 * q + 4, :].bitcast(I32),
                 )
 
         def load_weight(name, w):
@@ -59,21 +63,27 @@ def tile_picked_ycaser_relu_p_kernel(
             nc.sync.dma_start(out=tile[:], in_=rows[0, :].rearrange("(b p d) -> p b d", p=P, d=D))
             return tile
 
-        def interleave(name, raw, dealt):
-            width = raw.shape[2]
-            grouped = kept(name, [P, width * PACK], BF16)
-            order = "p (i c j) -> p c j i" if dealt else "p (c i j) -> p c j i"
-            nc.scalar.activation(
-                out=grouped[:].rearrange(order, i=4, j=PACK), in_=raw[:].rearrange("p j (c i) -> p c j i", i=4), func=COPY
-            )
-            return grouped
-
         def quantise(name, grouped):
             width = grouped.shape[1] // PACK
             codes = kept(name + "_codes", [P, width], U32)
             scales = kept(name + "_scales", [P, width], U8)
             nc.vector.quantize_mx(out=codes[:].bitcast(FP8X4), scales=scales[:], in_=grouped[:])
-            return codes, scales
+            return codes[:], scales[:]
+
+        def weight_views(name, raw, order):
+            grouped = kept(name + "_bf16", [P, raw.shape[2] * PACK], BF16)
+            run = LINE // 4
+            return grouped, grouped[:].rearrange(order, i=run, j=PACK), raw[:].rearrange("p j (c i) -> p c j i", i=run)
+
+        def tap_weight(name, raw):
+            grouped, dst, src = weight_views(name, raw, "p (i c j) -> p c j i")
+            nc.scalar.activation(out=dst, in_=src, func=COPY)
+            return quantise(name, grouped)
+
+        def head_weight(name, raw):
+            grouped, dst, src = weight_views(name, raw, "p (c i j) -> p c j i")
+            nc.gpsimd.tensor_scalar(out=dst, in0=src, scalar1=1.0, scalar2=0.0, op0=MULT, op1=ADD)
+            return quantise(name, grouped)
 
         def mx(dst, lhs, rhs, start, stop):
             nc.tensor.matmul_mx(
@@ -86,29 +96,30 @@ def tile_picked_ycaser_relu_p_kernel(
                 stop=stop,
             )
 
+        lead_words = LEAD // 4
         x_scale_tab = kept("x_scale_tab", [P, T], U8)
         e_scale_tab = kept("e_scale_tab", [P, W], U8)
-        x_got_words = kept("x_got_words", [P, LEAD_WORDS + S], U32)
-        x_got_scales = kept("x_got_scales", [P, LEAD_BYTES + S], U8)
+        x_got_words = kept("x_got_words", [P, lead_words + S], U32)
+        x_got_scales = kept("x_got_scales", [P, LEAD + S], U8)
         nc.gpsimd.memset(x_scale_tab[:].bitcast(I32), 0)
         nc.vector.memset(e_scale_tab[:].bitcast(I32), 0)
-        nc.vector.memset(x_got_words[:, :LEAD_WORDS].bitcast(I32), 0)
-        nc.vector.memset(x_got_scales[:, :LEAD_BYTES].bitcast(I32), 0)
+        nc.vector.memset(x_got_words[:, :lead_words].bitcast(I32), 0)
+        nc.vector.memset(x_got_scales[:, :LEAD].bitcast(I32), 0)
 
-        item_list = lists.tile([P, S // 16], U16, name="item_list")
-        user_list = lists.tile([P, V // 16], U16, name="user_list")
-        nc.sync.dma_start(item_list[:], offs)
+        item_list = lists.tile([P, S // LIST_ROWS], U16, name="item_list")
+        user_list = lists.tile([P, V // LIST_ROWS], U16, name="user_list")
         x_word_tab = load_words("x_word_tab", x_words, T)
-        load_scales(nc.sync, x_scale_tab, x_scales)
+        nc.sync.dma_start(item_list[:], offs)
+        load_scales(x_scale_tab, x_scales)
         w1_raw = load_weight("w1_raw", w1)
         w2_raw = load_weight("w2_raw", w2)
-        in1_col = load_factor("in1_col", in1)
-        pw_col = load_factor("pw_col", pw)
-        in2_col = load_factor("in2_col", in2)
-        nc.sync.dma_start(user_list[:], user)
         w3_raw = load_weight("w3_raw", w3)
+        in1_col = load_factor("in1_col", in1)
+        in2_col = load_factor("in2_col", in2)
+        pw_col = load_factor("pw_col", pw)
+        nc.sync.dma_start(user_list[:], user)
         e_word_tab = load_words("e_word_tab", e_words, W)
-        load_scales(nc.sync, e_scale_tab, e_scales)
+        load_scales(e_scale_tab, e_scales)
         w6_raw = load_weight("w6_raw", w6)
         w5_raw = load_weight("w5_raw", w5)
         w4_raw = load_weight("w4_raw", w4)
@@ -119,41 +130,29 @@ def tile_picked_ycaser_relu_p_kernel(
         make_identity(nc, eye_bf16[:])
 
         x_codes = kept("x_codes", [P, D + BACK, V], U32)
-        x_planes = kept("x_planes", [P, D + BACK, V], U8)
+        x_code_scales = kept("x_code_scales", [P, D + BACK, V], U8)
         for table, got, lead, dealt, run in (
-            (x_word_tab, x_got_words, LEAD_WORDS, x_codes, 4),
-            (x_scale_tab, x_got_scales, LEAD_BYTES, x_planes, 16),
+            (x_word_tab, x_got_words, lead_words, x_codes, LINE // 4),
+            (x_scale_tab, x_got_scales, LEAD, x_code_scales, LINE),
         ):
             nc.vector.tensor_copy(got[:, lead:], table[:].indirect(item_list[:]))
-            planes = dealt[:].rearrange("p e (c i) -> p c e i", i=run)
-            nc.vector.tensor_copy(planes[:, :, BACK:], got[:, lead:].rearrange("p (c i d) -> p c d i", i=run, d=D))
+            places = dealt[:].rearrange("p e (c i) -> p c e i", i=run)
+            nc.vector.tensor_copy(places[:, :, BACK:], got[:, lead:].rearrange("p (c i d) -> p c d i", i=run, d=D))
             earlier = got[:, lead - D : lead - D + S].rearrange("p (c i d) -> p c d i", i=run, d=D)
-            nc.vector.tensor_copy(planes[:, :, :BACK], earlier[:, :, D - BACK :])
-
-        taps = {}
-
-        def prepare(store, name, raw, dealt):
-            codes, scales = quantise(name, interleave(name + "_bf16", raw, dealt))
-            store[name] = (codes[:], scales[:])
+            nc.vector.tensor_copy(places[:, :, :BACK], earlier[:, :, D - BACK :])
 
         e_codes = kept("e_codes", [P, V], U32)
-        e_planes = kept("e_planes", [P, V], U8)
-        heads = {}
+        e_code_scales = kept("e_code_scales", [P, V], U8)
 
-        def by_slot(bank):
+        def product(weight, back, b, d):
+            users = slice(b * P, (b + 1) * P)
+            bank = psum.tile([P, H], F32, name=f"y{back}", bufs=TAP_BANKS)
+            row = d + BACK - back
+            mx(bank[:], (x_codes[:, row, users], x_code_scales[:, row, users]), weight, True, True)
             return bank[:].rearrange("p (t m) -> p t m", t=PACK)
 
-        def product(name, back, b, d):
-            users = slice(b * P, (b + 1) * P)
-            bank = psum.tile([P, H], F32, name=f"y{back}", bufs=2)
-            plane = d + BACK - back
-            mx(bank[:], (x_codes[:, plane, users], x_planes[:, plane, users]), taps[name], True, True)
-            return bank
-
-        def first_tap(b, d):
-            bank = product("w1", 0, b, d)
-            y0 = ring.tile([P, PACK, P], F32, name="y0_sb", bufs=5)
-            nc.scalar.activation(out=y0[:], in_=by_slot(bank), func=COPY)
+        def first_tap(b, d, y0):
+            nc.scalar.activation(out=y0[:], in_=product(w1_q, 0, b, d), func=COPY)
             return y0
 
         def weigh(b, d, y0):
@@ -162,18 +161,18 @@ def tile_picked_ycaser_relu_p_kernel(
             return yw
 
         def second_tap(b, d, y0):
-            bank = product("w2", 1, b, d)
-            y01 = ring.tile([P, PACK, P], F32, name="y01", bufs=4)
+            y1_bank = product(w2_q, 1, b, d)
+            y01 = ring.tile([P, PACK, P], F32, name="y01", bufs=AHEAD + 2)
             nc.vector.scalar_tensor_tensor(
-                out=y01[:], in0=by_slot(bank), scalar=in1_col[:, b, d : d + 1], in1=y0[:], op0=MULT, op1=ADD
+                out=y01[:], in0=y1_bank, scalar=in1_col[:, b, d : d + 1], in1=y0[:], op0=MULT, op1=ADD
             )
             return y01
 
         def third_tap(b, d, y01):
-            bank = product("w3", 2, b, d)
-            z = ring.tile([P, PACK, P], BF16, name="z", bufs=4)
+            y2_bank = product(w3_q, 2, b, d)
+            z = ring.tile([P, PACK, P], BF16, name="z", bufs=D)
             nc.vector.scalar_tensor_tensor(
-                out=z[:], in0=by_slot(bank), scalar=in2_col[:, b, d : d + 1], in1=y01[:], op0=MULT, op1=ADD
+                out=z[:], in0=y2_bank, scalar=in2_col[:, b, d : d + 1], in1=y01[:], op0=MULT, op1=ADD
             )
             return z
 
@@ -182,63 +181,68 @@ def tile_picked_ycaser_relu_p_kernel(
             nc.vector.tensor_tensor(out=larger[:], in0=best[:], in1=z[:], op=MAX)
             return larger
 
-        def add_turned(d, pair, vp_bank):
+        def add_turned(pair, vp_bank, opens, closes):
             turns = [(yw, t) for yw in pair for t in range(PACK)]
             for n, (yw, t) in enumerate(turns):
                 nc.tensor.matmul(
-                    vp_bank[:, t, :], yw[:, t, :], eye_f32[:],
-                    start=(d == 1 and n == 0), stop=(d == D - 1 and n == len(turns) - 1), is_transpose=True,
+                    vp_bank[:, t, :],
+                    yw[:, t, :],
+                    eye_f32[:],
+                    start=(opens and n == 0),
+                    stop=(closes and n == len(turns) - 1),
+                    is_transpose=True,
                 )
+
+        def interleaved(name, bank, func):
+            grouped = kept(name + "_bf16", [P, P * PACK], BF16)
+            nc.scalar.activation(
+                out=grouped[:].rearrange("p (v t) -> p v t", t=PACK), in_=bank[:].rearrange("p t v -> p v t"), func=func
+            )
+            return quantise(name, grouped)
 
         def head(b, best, vp_bank):
             users = slice(b * P, (b + 1) * P)
-            vp_bf16 = kept(f"vp_bf16_{b}", [P, P * PACK], BF16)
-            nc.scalar.activation(
-                out=vp_bf16[:].rearrange("p (v t) -> p v t", t=PACK), in_=vp_bank[:].rearrange("p t v -> p v t"), func=COPY
-            )
-            vp_q = quantise(f"vp{b}", vp_bf16)
+            vp_q = interleaved(f"vp{b}", vp_bank, COPY)
             out_bank = psum.tile([P, P], F32, name="vp")
-            mx(out_bank[:], heads["w6"], (e_codes[:, users], e_planes[:, users]), True, False)
-            mx(out_bank[:], heads["w5"], (vp_q[0][:], vp_q[1][:]), False, False)
-            hp_bank = psum.tile([P, PACK, P], BF16, name="tail")
+            mx(out_bank[:], w6_q, (e_codes[:, users], e_code_scales[:, users]), True, False)
+            mx(out_bank[:], w5_q, vp_q, False, False)
+            hp_bank = psum.tile([P, PACK, P], BF16, name="hp")
             for t in range(PACK):
                 nc.tensor.transpose(hp_bank[:, t, :], best[:, t, :], eye_bf16[:])
-            hp_bf16 = kept(f"hp_bf16_{b}", [P, P * PACK], BF16)
-            nc.scalar.activation(
-                out=hp_bf16[:].rearrange("p (v t) -> p v t", t=PACK), in_=hp_bank[:].rearrange("p t v -> p v t"), func=RELU
-            )
-            hp_q = quantise(f"hp{b}", hp_bf16)
-            mx(out_bank[:], heads["w4"], (hp_q[0][:], hp_q[1][:]), False, True)
+            mx(out_bank[:], w4_q, interleaved(f"hp{b}", hp_bank, RELU), False, True)
             result = kept(f"result{b}", [P, P], F32)
             nc.scalar.activation(out=result[:], in_=out_bank[:], func=RELU)
             nc.sync.dma_start(out=out[:, users], in_=result[:])
 
+        w1_q = tap_weight("w1", w1_raw)
+        w2_q = tap_weight("w2", w2_raw)
+        w3_q = tap_weight("w3", w3_raw)
+
         steps = [(b, d) for b in range(BLOCKS) for d in range(D)]
-        prepare(taps, "w1", w1_raw, True)
-        prepare(taps, "w2", w2_raw, True)
-        nc.vector.tensor_copy(e_codes[:], e_word_tab[:].indirect(user_list[:]))
-        nc.vector.tensor_copy(e_planes[:], e_scale_tab[:].indirect(user_list[:]))
-        prepare(taps, "w3", w3_raw, True)
-        firsts = [first_tap(*steps[n]) for n in range(2)]
-        seconds = [second_tap(*steps[n], firsts[n]) for n in range(2)]
+        firsts = [
+            first_tap(*steps[n], keep.tile([P, PACK, P], F32, name="y0_early", tag=tag, align_bytes=64))
+            for n, tag in enumerate(("w2_raw", "w3_raw"))
+        ]
+        seconds = [second_tap(*steps[n], firsts[n]) for n in range(AHEAD)]
         weighed = []
-        thirds = []
-        best = None
-        vp_bank = None
         for n, (b, d) in enumerate(steps):
-            if n + 2 < len(steps):
-                firsts.append(first_tap(*steps[n + 2]))
+            ahead = n + AHEAD
+            if ahead < len(steps):
+                firsts.append(first_tap(*steps[ahead], ring.tile([P, PACK, P], F32, name="y0", bufs=AHEAD + 2)))
             weighed.append(weigh(b, d, firsts[n]))
             if d == 1:
                 vp_bank = psum.tile([P, PACK, P], F32, name="vp")
             if d % 2 == 1:
-                add_turned(d, (weighed[n], weighed[n - 1]), vp_bank)
-            thirds.append(third_tap(b, d, seconds[n]))
-            if n + 2 < len(steps):
-                seconds.append(second_tap(*steps[n + 2], firsts[n + 2]))
-            best = thirds[n] if d == 0 else larger_of(best, thirds[n])
+                add_turned((weighed[n], weighed[n - 1]), vp_bank, opens=(d == 1), closes=(d == D - 1))
+            z = third_tap(b, d, seconds[n])
+            if ahead < len(steps):
+                seconds.append(second_tap(*steps[ahead], firsts[ahead]))
+            best = z if d == 0 else larger_of(best, z)
             if n == 1:
-                for name, raw in (("w6", w6_raw), ("w5", w5_raw), ("w4", w4_raw)):
-                    prepare(heads, name, raw, False)
+                nc.vector.tensor_copy(e_codes[:], e_word_tab[:].indirect(user_list[:]))
+                nc.vector.tensor_copy(e_code_scales[:], e_scale_tab[:].indirect(user_list[:]))
+                w6_q = head_weight("w6", w6_raw)
+                w5_q = head_weight("w5", w5_raw)
+                w4_q = head_weight("w4", w4_raw)
             if d == D - 1:
                 head(b, best, vp_bank)

from contextlib import ExitStack

import concourse.mybir as mybir
from concourse.masks import make_identity

K, T, S, D, H, N, V, W = 512, 2048, 1024, 4, 512, 128, 256, 1024
FLOPS = 2 * (3 * K * H * S + 2 * H * N * V + K * N * V)

F32 = mybir.dt.float32
BF16 = mybir.dt.bfloat16
I32 = mybir.dt.int32
U32 = mybir.dt.uint32
U16 = mybir.dt.uint16
U8 = mybir.dt.uint8
FP8X4 = mybir.dt.float8_e4m3fn_x4
MULT, ADD, MAX = mybir.AluOpType.mult, mybir.AluOpType.add, mybir.AluOpType.max
COPY, RELU = mybir.ActivationFunctionType.Copy, mybir.ActivationFunctionType.Relu

P = 128
PACK = 4
QUADRANT = 32
LIST_ROWS = 16
BACK = 2
BLOCKS = V // P
LINE = 16
LEAD = 32
AHEAD = 2
TAP_BANKS = 2


def tile_picked_ycaser_relu_p_kernel(
    tc, x_words, x_scales, e_words, e_scales, w1, w2, w3, in1, in2, pw, w4, w5, w6, offs, user, out
):
    nc = tc.nc
    with ExitStack() as ctx:
        lists = ctx.enter_context(tc.tile_pool(name="lists", bufs=1))
        keep = ctx.enter_context(tc.tile_pool(name="keep", bufs=1))
        ring = ctx.enter_context(tc.tile_pool(name="ring", bufs=3))
        psum = ctx.enter_context(tc.psum_pool(name="psum", bufs=1))

        def kept(name, shape, dtype):
            return keep.tile(shape, dtype, name=name, tag=name, align_bytes=64)

        def load_words(name, words, width):
            tile = kept(name, [P, width], U32)
            nc.sync.dma_start(out=tile[:].bitcast(I32), in_=words[0].rearrange("p n t -> p (n t)").bitcast(I32))
            return tile

        def load_scales(tile, scales):
            for q in range(P // QUADRANT):
                nc.sync.dma_start(
                    out=tile[QUADRANT * q : QUADRANT * q + 4, :].bitcast(I32),
                    in_=scales[0, 4 * q : 4 * q + 4, :].bitcast(I32),
                )

        def load_weight(name, w):
            tile = kept(name, [P, PACK, w.shape[1]], F32)
            nc.sync.dma_start(out=tile[:], in_=w.rearrange("(p j) c -> p j c", j=PACK))
            return tile

        def load_factor(name, rows):
            tile = kept(name, [P, BLOCKS, D], F32)
            nc.sync.dma_start(out=tile[:], in_=rows[0, :].rearrange("(b p d) -> p b d", p=P, d=D))
            return tile

        def quantise(name, grouped):
            width = grouped.shape[1] // PACK
            codes = kept(name + "_codes", [P, width], U32)
            scales = kept(name + "_scales", [P, width], U8)
            nc.vector.quantize_mx(out=codes[:].bitcast(FP8X4), scales=scales[:], in_=grouped[:])
            return codes[:], scales[:]

        def weight_views(name, raw, order):
            grouped = kept(name + "_bf16", [P, raw.shape[2] * PACK], BF16)
            run = LINE // 4
            return grouped, grouped[:].rearrange(order, i=run, j=PACK), raw[:].rearrange("p j (c i) -> p c j i", i=run)

        def tap_weight(name, raw):
            grouped, dst, src = weight_views(name, raw, "p (i c j) -> p c j i")
            nc.scalar.activation(out=dst, in_=src, func=COPY)
            return quantise(name, grouped)

        def head_weight(name, raw):
            grouped, dst, src = weight_views(name, raw, "p (c i j) -> p c j i")
            nc.gpsimd.tensor_scalar(out=dst, in0=src, scalar1=1.0, scalar2=0.0, op0=MULT, op1=ADD)
            return quantise(name, grouped)

        def mx(dst, lhs, rhs, start, stop):
            nc.tensor.matmul_mx(
                out=dst,
                lhsT=lhs[0].bitcast(FP8X4),
                lhsT_scale=lhs[1],
                rhs=rhs[0].bitcast(FP8X4),
                rhs_scale=rhs[1],
                start=start,
                stop=stop,
            )

        lead_words = LEAD // 4
        x_scale_tab = kept("x_scale_tab", [P, T], U8)
        e_scale_tab = kept("e_scale_tab", [P, W], U8)
        x_got_words = kept("x_got_words", [P, lead_words + S], U32)
        x_got_scales = kept("x_got_scales", [P, LEAD + S], U8)
        nc.gpsimd.memset(x_scale_tab[:].bitcast(I32), 0)
        nc.vector.memset(e_scale_tab[:].bitcast(I32), 0)
        nc.vector.memset(x_got_words[:, :lead_words].bitcast(I32), 0)
        nc.vector.memset(x_got_scales[:, :LEAD].bitcast(I32), 0)

        item_list = lists.tile([P, S // LIST_ROWS], U16, name="item_list")
        user_list = lists.tile([P, V // LIST_ROWS], U16, name="user_list")
        x_word_tab = load_words("x_word_tab", x_words, T)
        nc.sync.dma_start(item_list[:], offs)
        load_scales(x_scale_tab, x_scales)
        w1_raw = load_weight("w1_raw", w1)
        w2_raw = load_weight("w2_raw", w2)
        w3_raw = load_weight("w3_raw", w3)
        in1_col = load_factor("in1_col", in1)
        in2_col = load_factor("in2_col", in2)
        pw_col = load_factor("pw_col", pw)
        nc.sync.dma_start(user_list[:], user)
        e_word_tab = load_words("e_word_tab", e_words, W)
        load_scales(e_scale_tab, e_scales)
        w6_raw = load_weight("w6_raw", w6)
        w5_raw = load_weight("w5_raw", w5)
        w4_raw = load_weight("w4_raw", w4)

        eye_f32 = kept("eye_f32", [P, P], F32)
        eye_bf16 = kept("eye_bf16", [P, P], BF16)
        make_identity(nc, eye_f32[:])
        make_identity(nc, eye_bf16[:])

        x_codes = kept("x_codes", [P, D + BACK, V], U32)
        x_code_scales = kept("x_code_scales", [P, D + BACK, V], U8)
        for table, got, lead, dealt, run in (
            (x_word_tab, x_got_words, lead_words, x_codes, LINE // 4),
            (x_scale_tab, x_got_scales, LEAD, x_code_scales, LINE),
        ):
            nc.vector.tensor_copy(got[:, lead:], table[:].indirect(item_list[:]))
            places = dealt[:].rearrange("p e (c i) -> p c e i", i=run)
            nc.vector.tensor_copy(places[:, :, BACK:], got[:, lead:].rearrange("p (c i d) -> p c d i", i=run, d=D))
            earlier = got[:, lead - D : lead - D + S].rearrange("p (c i d) -> p c d i", i=run, d=D)
            nc.vector.tensor_copy(places[:, :, :BACK], earlier[:, :, D - BACK :])

        e_codes = kept("e_codes", [P, V], U32)
        e_code_scales = kept("e_code_scales", [P, V], U8)

        def product(weight, back, b, d):
            users = slice(b * P, (b + 1) * P)
            bank = psum.tile([P, H], F32, name=f"y{back}", bufs=TAP_BANKS)
            row = d + BACK - back
            mx(bank[:], (x_codes[:, row, users], x_code_scales[:, row, users]), weight, True, True)
            return bank[:].rearrange("p (t m) -> p t m", t=PACK)

        def first_tap(b, d, y0):
            nc.scalar.activation(out=y0[:], in_=product(w1_q, 0, b, d), func=COPY)
            return y0

        def weigh(b, d, y0):
            yw = ring.tile([P, PACK, P], F32, name="yw", bufs=4)
            nc.scalar.activation(out=yw[:], in_=y0[:], func=COPY, scale=pw_col[:, b, d : d + 1])
            return yw

        def second_tap(b, d, y0):
            y1_bank = product(w2_q, 1, b, d)
            y01 = ring.tile([P, PACK, P], F32, name="y01", bufs=AHEAD + 2)
            nc.vector.scalar_tensor_tensor(
                out=y01[:], in0=y1_bank, scalar=in1_col[:, b, d : d + 1], in1=y0[:], op0=MULT, op1=ADD
            )
            return y01

        def third_tap(b, d, y01):
            y2_bank = product(w3_q, 2, b, d)
            z = ring.tile([P, PACK, P], BF16, name="z", bufs=D)
            nc.vector.scalar_tensor_tensor(
                out=z[:], in0=y2_bank, scalar=in2_col[:, b, d : d + 1], in1=y01[:], op0=MULT, op1=ADD
            )
            return z

        def larger_of(best, z):
            larger = ring.tile([P, PACK, P], BF16, name="larger")
            nc.vector.tensor_tensor(out=larger[:], in0=best[:], in1=z[:], op=MAX)
            return larger

        def add_turned(pair, vp_bank, opens, closes):
            turns = [(yw, t) for yw in pair for t in range(PACK)]
            for n, (yw, t) in enumerate(turns):
                nc.tensor.matmul(
                    vp_bank[:, t, :],
                    yw[:, t, :],
                    eye_f32[:],
                    start=(opens and n == 0),
                    stop=(closes and n == len(turns) - 1),
                    is_transpose=True,
                )

        def interleaved(name, bank, func):
            grouped = kept(name + "_bf16", [P, P * PACK], BF16)
            nc.scalar.activation(
                out=grouped[:].rearrange("p (v t) -> p v t", t=PACK), in_=bank[:].rearrange("p t v -> p v t"), func=func
            )
            return quantise(name, grouped)

        def head(b, best, vp_bank):
            users = slice(b * P, (b + 1) * P)
            vp_q = interleaved(f"vp{b}", vp_bank, COPY)
            out_bank = psum.tile([P, P], F32, name="vp")
            mx(out_bank[:], w6_q, (e_codes[:, users], e_code_scales[:, users]), True, False)
            mx(out_bank[:], w5_q, vp_q, False, False)
            hp_bank = psum.tile([P, PACK, P], BF16, name="hp")
            for t in range(PACK):
                nc.tensor.transpose(hp_bank[:, t, :], best[:, t, :], eye_bf16[:])
            mx(out_bank[:], w4_q, interleaved(f"hp{b}", hp_bank, RELU), False, True)
            result = kept(f"result{b}", [P, P], F32)
            nc.scalar.activation(out=result[:], in_=out_bank[:], func=RELU)
            nc.sync.dma_start(out=out[:, users], in_=result[:])

        w1_q = tap_weight("w1", w1_raw)
        w2_q = tap_weight("w2", w2_raw)
        w3_q = tap_weight("w3", w3_raw)

        steps = [(b, d) for b in range(BLOCKS) for d in range(D)]
        firsts = [
            first_tap(*steps[n], keep.tile([P, PACK, P], F32, name="y0_early", tag=tag, align_bytes=64))
            for n, tag in enumerate(("w2_raw", "w3_raw"))
        ]
        seconds = [second_tap(*steps[n], firsts[n]) for n in range(AHEAD)]
        weighed = []
        for n, (b, d) in enumerate(steps):
            ahead = n + AHEAD
            if ahead < len(steps):
                firsts.append(first_tap(*steps[ahead], ring.tile([P, PACK, P], F32, name="y0", bufs=AHEAD + 2)))
            weighed.append(weigh(b, d, firsts[n]))
            if d == 1:
                vp_bank = psum.tile([P, PACK, P], F32, name="vp")
            if d % 2 == 1:
                add_turned((weighed[n], weighed[n - 1]), vp_bank, opens=(d == 1), closes=(d == D - 1))
            z = third_tap(b, d, seconds[n])
            if ahead < len(steps):
                seconds.append(second_tap(*steps[ahead], firsts[ahead]))
            best = z if d == 0 else larger_of(best, z)
            if n == 1:
                nc.vector.tensor_copy(e_codes[:], e_word_tab[:].indirect(user_list[:]))
                nc.vector.tensor_copy(e_code_scales[:], e_scale_tab[:].indirect(user_list[:]))
                w6_q = head_weight("w6", w6_raw)
                w5_q = head_weight("w5", w5_raw)
                w4_q = head_weight("w4", w4_raw)
            if d == D - 1:
                head(b, best, vp_bank)
